import numpy as np
import ml_dtypes


def mxq(x, axis, fmt="e4m3"):
    dtype, down = {"e4m3": (ml_dtypes.float8_e4m3fn, 7), "e5m2": (ml_dtypes.float8_e5m2, 14)}[fmt]
    v = np.moveaxis(np.asarray(x, np.float32).astype(ml_dtypes.bfloat16).astype(np.float64), axis, -1)
    blocks = v.reshape(v.shape[:-1] + (-1, 32))
    amax = np.abs(blocks).max(-1, keepdims=True)
    byte = np.maximum(np.where(amax > 0, np.frexp(amax)[1] - 1 + 127, 0) - down, 1)
    scale = np.exp2(byte - 127.0)
    codes = (blocks / scale).astype(np.float32).astype(dtype).astype(np.float64)
    return np.moveaxis((codes * scale).reshape(v.shape), -1, axis)


WIDE = False


def mx_kscale(k):
    if not WIDE:
        return np.ones(k)
    levels = np.array([10, -10, 5, -5, 0])
    if k % 512:
        return np.exp2(np.random.permutation(np.resize(levels, k // 32))).repeat(32)
    a = np.empty((k // 512, 16))
    for p in range(k // 512):
        a[p, :8] = np.random.permutation(np.resize(levels, 8))
        for g in range(8):
            far = levels[np.abs(levels - a[p, g]) >= 10]
            a[p, g + 8] = far[np.random.randint(len(far))]
    return np.exp2(a.ravel()).repeat(32)


def f64(x):
    return np.asarray(x).astype(np.float64)


def striped(idx):
    return np.tile(idx.reshape(-1, 16).T, (8, 1)).astype(np.uint16)


def unstriped(offs):
    return offs[:16].T.reshape(-1).astype(np.int64)


def striped8(idx):
    return np.concatenate([x.reshape(-1, 16).T for x in idx]).astype(np.uint16)


def runs(offs, k):
    lists = np.stack([offs[16 * r : 16 * r + 16].T.reshape(-1) for r in range(8)]).astype(np.int64)
    return lists[np.arange(k) % 512 // 64]


def pack_weight(w):
    k, n = w.shape
    w = f64(np.asarray(w, np.float32).astype(ml_dtypes.bfloat16)).reshape(k // 32, 32, n)
    amax = np.abs(w).max(1)
    byte = np.clip(np.where(amax > 0, np.frexp(amax)[1] - 1 + 127 - 7, 1), 1, 254)
    scaled = (w * np.exp2(127.0 - byte)[:, None, :]).reshape(k, n).astype(np.float32)
    words = np.ascontiguousarray(scaled.reshape(k // 512, 128, 4, n).transpose(0, 1, 3, 2)).astype(ml_dtypes.float8_e4m3fn).view(np.uint8)
    return words, np.ascontiguousarray(byte.astype(np.uint8).reshape(k // 512, 16, n))


def unpack_weight(words, scales):
    g, p, n, _ = words.shape
    vals = np.ascontiguousarray(words).view(ml_dtypes.float8_e4m3fn).astype(np.float64) * np.repeat(np.exp2(scales.astype(np.float64) - 127.0), 8, axis=1)[..., None]
    return vals.transpose(0, 1, 3, 2).reshape(g * 512, n)

def planes(y):
    n, m = y.shape
    v = y.astype(np.float32).astype(ml_dtypes.bfloat16).astype(np.float64).reshape(n // 32, 32, m)
    top = np.abs(v).max(1)
    byte = np.clip(np.where(top > 0, np.frexp(top)[1] - 1 + 127 - 7, 1), 1, 254)
    codes = (v * np.exp2(127.0 - byte)[:, None, :]).reshape(n, m).astype(np.float32).astype(ml_dtypes.float8_e4m3fn).view(np.uint8)
    words = codes.reshape(n // 512, 128, 4, m).transpose(0, 1, 3, 2)
    return np.ascontiguousarray(words), np.ascontiguousarray(byte.astype(np.uint8).reshape(n // 512, 16, m))


K, T, S, N, H = 512, 2048, 512, 512, 512


def setup_inputs():
    n = np.random.standard_normal
    s = mx_kscale(K)[:, None]
    u = mx_kscale(S)
    packed_xT = pack_weight(n((K, T)) * s)
    packed_w1 = pack_weight(n((S, N)) / np.sqrt(S) / u[:, None])
    return {
        "x_words": packed_xT[0],
        "x_scales": packed_xT[1],
        "wa": (n((K, H)) / np.sqrt(K) / s).astype(np.float32),
        "gt": (np.random.uniform(0.5, 1.5, (S, 1)) * u[:, None]).astype(np.float32),
        "w1_words": packed_w1[0],
        "w1_scales": packed_w1[1],
        "offs": striped(np.random.permutation(T)[:S]),
        "n1": striped8(np.stack([np.random.permutation(H) for _ in range(8)])),
        "n2": striped8(np.stack([np.random.permutation(H) for _ in range(8)])),
        "n3": striped8(np.stack([np.random.permutation(H) for _ in range(8)])),
        "n4": striped8(np.stack([np.random.permutation(H) for _ in range(8)])),
    }


def reference(x_words, x_scales, wa, gt, w1_words, w1_scales, offs, n1, n2, n3, n4):
    xq = unpack_weight(x_words, x_scales)[:, unstriped(offs)]
    y = xq.T @ mxq(f64(wa), 0, "e4m3")
    z = f64(gt) * ((np.tanh(y[np.arange(S)[:, None], runs(n1, S)] - y)) * (y[np.arange(S)[:, None], runs(n2, S)]))
    h = unpack_weight(w1_words, w1_scales).T @ mxq(z, 0, "e4m3")
    out_0 = h[np.arange(N)[:, None], runs(n3, N)] + 0.75 * (h[np.arange(N)[:, None], runs(n4, N)])
    return (out_0,) + planes(out_0)

@@ -1,0 +1,192 @@
+from contextlib import ExitStack
+
+import concourse.mybir as mybir
+
+F32 = mybir.dt.float32
+BF16 = mybir.dt.bfloat16
+U32 = mybir.dt.uint32
+I32 = mybir.dt.int32
+U16 = mybir.dt.uint16
+U8 = mybir.dt.uint8
+FP8X4 = mybir.dt.float8_e4m3fn_x4
+ALU = mybir.AluOpType
+ACT = mybir.ActivationFunctionType
+
+K, T, S, N, H = 512, 2048, 512, 512, 512
+P = 128
+PACK = 4
+FLOPS = 2 * K * S * H + 2 * S * N * H
+
+WA_CHUNKS = [(0, 128), (128, 256), (256, 384), (384, 512)]
+HALVES = [(0, 256), (256, 512)]
+CHUNKS = [(0, 256), (256, 384), (384, 512)]
+
+
+def entries(lst, c0, c1):
+    return lst[:, c0 // 16 : c1 // 16]
+
+
+def load_scale_rows(queue, tile, rows):
+    for q in range(4):
+        queue.dma_start(out=tile[32 * q : 32 * q + 4, :].bitcast(I32), in_=rows[4 * q : 4 * q + 4, :].bitcast(I32))
+
+
+def tile_picked_tokfdifsum_none_po_kernel(tc, x_words, x_scales, wa, gt, w1_words, w1_scales, offs, n1, n2, n3, n4, out_0, out_1, out_2):
+    nc = tc.nc
+    with ExitStack() as ctx:
+        sb = ctx.enter_context(tc.tile_pool(name="sb", bufs=1))
+        ps = ctx.enter_context(tc.psum_pool(name="ps", bufs=1))
+
+        def tile(name, shape, dtype):
+            return sb.tile(shape, dtype, name=name, align_bytes=64)
+
+        offs_t = tile("offs_t", [P, S // 16], U16)
+        n1_t = tile("n1_t", [P, H // 16], U16)
+        n2_t = tile("n2_t", [P, H // 16], U16)
+        n3_t = tile("n3_t", [P, H // 16], U16)
+        n4_t = tile("n4_t", [P, H // 16], U16)
+
+        xs = tile("xs", [P, T], U8)
+        w1s = tile("w1s", [P, N], U8)
+        zero = tile("zero", [P, 1], F32)
+        tanh_bias = tile("tanh_bias", [P, 1], F32)
+        nc.vector.memset(xs[:].bitcast(I32), 0)
+        nc.vector.memset(zero[:], 0.0)
+        nc.scalar.activation(tanh_bias[:], zero[:], ACT.Tanh)
+        nc.vector.memset(w1s[:].bitcast(I32), 0)
+
+        wa_rows = wa.rearrange("(p j) c -> p j c", j=PACK)
+        wa_raw = [tile(f"wa_raw{i}", [P, PACK, c1 - c0], F32) for i, (c0, c1) in enumerate(WA_CHUNKS)]
+        xw = tile("xw", [P, T], U32)
+        w1w = tile("w1w", [P, N], U32)
+        gt_t = tile("gt_t", [P, PACK], F32)
+
+        nc.sync.dma_start(offs_t[:], offs)
+        nc.sync.dma_start(out=wa_raw[0][:], in_=wa_rows[:, :, WA_CHUNKS[0][0] : WA_CHUNKS[0][1]])
+        load_scale_rows(nc.sync, xs, x_scales[0])
+        nc.sync.dma_start(out=xw[:].bitcast(I32), in_=x_words[0].rearrange("p n t -> p (n t)").bitcast(I32))
+        for i in range(1, len(WA_CHUNKS)):
+            nc.sync.dma_start(out=wa_raw[i][:], in_=wa_rows[:, :, WA_CHUNKS[i][0] : WA_CHUNKS[i][1]])
+        nc.sync.dma_start(n1_t[:], n1)
+        nc.sync.dma_start(out=w1w[:].bitcast(I32), in_=w1_words[0].rearrange("p n t -> p (n t)").bitcast(I32))
+        load_scale_rows(nc.sync, w1s, w1_scales[0])
+        nc.sync.dma_start(out=gt_t[:], in_=gt.rearrange("(p t) o -> p (t o)", t=PACK))
+        nc.sync.dma_start(n2_t[:], n2)
+        nc.sync.dma_start(n4_t[:], n4)
+        nc.sync.dma_start(n3_t[:], n3)
+
+        xsg = tile("xsg", [P, S], U8)
+        xsd = tile("xsd", [P, PACK, P], U8)
+        xg = tile("xg", [P, PACK, P], U32)
+        nc.vector.tensor_copy(xsg[:], xs[:].indirect(offs_t[:]))
+        nc.vector.tensor_copy(xsd[:].rearrange("p t s -> p s t"), xsg[:].rearrange("p (s t) -> p s t", t=PACK))
+        nc.vector.tensor_copy(xg[:].rearrange("p t s -> p s t"), xw[:].indirect(offs_t[:]))
+
+        wa_q = tile("wa_q", [P, H], U32)
+        wa_s = tile("wa_s", [P, H], U8)
+        y_ps = [ps.tile([P, H], F32, name=f"y_ps{t}", tag=f"bank{t}") for t in range(PACK)]
+        for i, (c0, c1) in enumerate(WA_CHUNKS):
+            wa_bf = tile(f"wa_bf{i}", [P, c1 - c0, PACK], BF16)
+            src = wa_raw[i][:].rearrange("p j c -> p c j")
+            if i == len(WA_CHUNKS) - 1:
+                nc.vector.tensor_copy(wa_bf[:], src)
+            else:
+                nc.scalar.copy(wa_bf[:], src)
+            nc.vector.quantize_mx(out=wa_q[:, c0:c1].bitcast(FP8X4), scales=wa_s[:, c0:c1], in_=wa_bf[:].rearrange("p c j -> p (c j)"))
+            nc.tensor.matmul_mx(out=y_ps[0][:, c0:c1], lhsT=xg[:, 0, :].bitcast(FP8X4), lhsT_scale=xsd[:, 0, :],
+                                rhs=wa_q[:, c0:c1].bitcast(FP8X4), rhs_scale=wa_s[:, c0:c1], start=True, stop=True)
+        for t in range(1, PACK):
+            nc.tensor.matmul_mx(out=y_ps[t][:], lhsT=xg[:, t, :].bitcast(FP8X4), lhsT_scale=xsd[:, t, :],
+                                rhs=wa_q[:].bitcast(FP8X4), rhs_scale=wa_s[:], start=True, stop=True)
+
+        w1wd = tile("w1wd", [P, PACK, P], U32)
+        w1sd = tile("w1sd", [P, PACK, P], U8)
+        nc.vector.tensor_copy(w1wd[:].bitcast(I32).rearrange("p t s -> p s t"), w1w[:].bitcast(I32).rearrange("p (s t) -> p s t", t=PACK))
+        nc.vector.tensor_copy(w1sd[:].rearrange("p t s -> p s t"), w1s[:].rearrange("p (s t) -> p s t", t=PACK))
+
+        y = [tile(f"y{t}", [P, H], F32) for t in range(PACK)]
+        y2 = [tile(f"y2_{t}", [P, H], F32) for t in range(PACK)]
+        gy = [tile(f"gy{t}", [P, H], F32) for t in range(PACK)]
+        d = [tile(f"d{t}", [P, H], F32) for t in range(PACK)]
+        th = [tile(f"th{t}", [P, H], F32) for t in range(PACK)]
+        for t in range(PACK):
+            nc.scalar.copy(y[t][:], y_ps[t][:])
+        for t in range(PACK):
+            nc.vector.tensor_copy(y2[t][:], y[t][:])
+            for c0, c1 in HALVES:
+                nc.vector.tensor_tensor(d[t][:, c0:c1], y[t][:].indirect(entries(n1_t, c0, c1)), y2[t][:, c0:c1], ALU.subtract)
+        for t in range(PACK):
+            nc.scalar.activation(gy[t][:], y[t][:], ACT.Copy, scale=gt_t[:, t : t + 1])
+            nc.scalar.activation(th[t][:], d[t][:], ACT.Tanh, bias=tanh_bias[:])
+
+        z_q = tile("z_q", [P, H], U32)
+        z_s = tile("z_s", [P, H], U8)
+        h = [tile(f"h{t}", [P, H], F32) for t in range(PACK)]
+        ha = [ps.tile([P, 2, 256], F32, name=f"ha{u}", tag=f"bank{4 + u}") for u in range(2)]
+        hb = ps.tile([P, PACK, 128], F32, name="hb", tag="bank6")
+        hc = [ps.tile([P, 128], F32, name=f"hc{t}", tag=f"bank{t}") for t in range(PACK)]
+        h_ps = [[ha[t // 2][:, t % 2, :] for t in range(PACK)], [hb[:, t, :] for t in range(PACK)], [hc[t][:] for t in range(PACK)]]
+
+        z = [tile(f"z{i}", [P, PACK, c1 - c0], F32) for i, (c0, c1) in enumerate(CHUNKS)]
+        z_bf = [tile(f"z_bf{i}", [P, c1 - c0, PACK], BF16) for i, (c0, c1) in enumerate(CHUNKS)]
+
+        def finish_z(i):
+            c0, c1 = CHUNKS[i]
+            nc.vector.quantize_mx(out=z_q[:, c0:c1].bitcast(FP8X4), scales=z_s[:, c0:c1], in_=z_bf[i][:].rearrange("p c j -> p (c j)"))
+            for t in range(PACK):
+                nc.tensor.matmul_mx(out=h_ps[i][t], lhsT=w1wd[:, t, :].bitcast(FP8X4), lhsT_scale=w1sd[:, t, :],
+                                    rhs=z_q[:, c0:c1].bitcast(FP8X4), rhs_scale=z_s[:, c0:c1], start=True, stop=True)
+
+        last = len(CHUNKS) - 1
+        for i, (c0, c1) in enumerate(CHUNKS):
+            for t in range(PACK):
+                nc.vector.tensor_tensor(z[i][:, t, :], gy[t][:].indirect(entries(n2_t, c0, c1)), th[t][:, c0:c1], ALU.mult)
+            src = z[i][:].rearrange("p j c -> p c j")
+            if i > 0:
+                finish_z(i - 1)
+            if i == last:
+                nc.vector.tensor_copy(z_bf[i][:], src)
+            else:
+                nc.scalar.copy(z_bf[i][:], src)
+        finish_z(last)
+        for t in range(PACK):
+            for i, (c0, c1) in enumerate(CHUNKS):
+                nc.scalar.copy(h[t][:, c0:c1], h_ps[i][t])
+
+        o_q = tile("o_q", [P, H], U32)
+        o_s = tile("o_s", [P, H], U8)
+        out_rows = out_0.rearrange("(p t) j -> p t j", t=PACK)
+        out_words = out_1[0].rearrange("p n t -> p (n t)").bitcast(I32)
+        o = [tile(f"o{i}", [P, PACK, c1 - c0], F32) for i, (c0, c1) in enumerate(CHUNKS)]
+        o_bf = [tile(f"o_bf{i}", [P, c1 - c0, PACK], BF16) for i, (c0, c1) in enumerate(CHUNKS)]
+        g = [tile(f"g{i}", [P, PACK, c1 - c0], F32) for i, (c0, c1) in enumerate(CHUNKS)]
+
+        def finish_o(i):
+            c0, c1 = CHUNKS[i]
+            nc.vector.quantize_mx(out=o_q[:, c0:c1].bitcast(FP8X4), scales=o_s[:, c0:c1], in_=o_bf[i][:].rearrange("p c j -> p (c j)"))
+            nc.sync.dma_start(out=out_words[:, c0:c1], in_=o_q[:, c0:c1].bitcast(I32))
+
+        for i, (c0, c1) in enumerate(CHUNKS):
+            def first(t):
+                nc.vector.tensor_scalar(g[i][:, t, :], h[t][:].indirect(entries(n4_t, c0, c1)), 0.75, 0.0, ALU.mult, ALU.add)
+
+            def second(t):
+                nc.vector.tensor_tensor(o[i][:, t, :], h[t][:].indirect(entries(n3_t, c0, c1)), g[i][:, t, :], ALU.add)
+
+            first(0)
+            for t in range(1, PACK):
+                first(t)
+                second(t - 1)
+            if i > 0:
+                finish_o(i - 1)
+            second(PACK - 1)
+            nc.sync.dma_start(out=out_rows[:, :, c0:c1], in_=o[i][:])
+            src = o[i][:].rearrange("p j c -> p c j")
+            if i == last:
+                nc.vector.tensor_copy(o_bf[i][:], src)
+            else:
+                nc.scalar.copy(o_bf[i][:], src)
+        finish_o(last)
+        for q in range(4):
+            queue = nc.scalar if q < 2 else nc.sync
+            queue.dma_start(out=out_2[0, 4 * q : 4 * q + 4, :].bitcast(I32), in_=o_s[32 * q : 32 * q + 4, :].bitcast(I32))

@@ -18,8 +18,8 @@ PACK = 4
 FLOPS = 2 * K * S * H + 2 * S * N * H
 
 WA_CHUNKS = [(0, 128), (128, 256), (256, 384), (384, 512)]
-HALVES = [(0, 256), (256, 512)]
 CHUNKS = [(0, 256), (256, 384), (384, 512)]
+TAIL = 384
 
 
 def entries(lst, c0, c1):
@@ -27,8 +27,12 @@ def entries(lst, c0, c1):
 
 
 def load_scale_rows(queue, tile, rows):
-    for q in range(4):
-        queue.dma_start(out=tile[32 * q : 32 * q + 4, :].bitcast(I32), in_=rows[4 * q : 4 * q + 4, :].bitcast(I32))
+    for r in range(4):
+        queue.dma_start(out=tile[r:P:32, :].bitcast(I32), in_=rows[r:16:4, :].bitcast(I32))
+
+
+def interleave(copy, dst, src):
+    copy(dst[:].rearrange("p (c i) t -> p c t i", i=4), src[:].rearrange("p t (c i) -> p c t i", i=4))
 
 
 def tile_picked_tokfdifsum_none_po_kernel(tc, x_words, x_scales, wa, gt, w1_words, w1_scales, offs, n1, n2, n3, n4, out_0, out_1, out_2):
@@ -37,8 +41,14 @@ def tile_picked_tokfdifsum_none_po_kernel(tc, x_words, x_scales, wa, gt, w1_word
         sb = ctx.enter_context(tc.tile_pool(name="sb", bufs=1))
         ps = ctx.enter_context(tc.psum_pool(name="ps", bufs=1))
 
-        def tile(name, shape, dtype):
-            return sb.tile(shape, dtype, name=name, align_bytes=64)
+        def tile(name, shape, dtype, tag=""):
+            return sb.tile(shape, dtype, name=name, align_bytes=64, tag=tag or name)
+
+        def mx(out, lhs_q, lhs_s, rhs_q, rhs_s):
+            nc.tensor.matmul_mx(out=out, lhsT=lhs_q.bitcast(FP8X4), lhsT_scale=lhs_s, rhs=rhs_q.bitcast(FP8X4), rhs_scale=rhs_s, start=True, stop=True)
+
+        def quantize(codes, scales, src):
+            nc.vector.quantize_mx(out=codes.bitcast(FP8X4), scales=scales, in_=src[:].rearrange("p c t -> p (c t)"))
 
         offs_t = tile("offs_t", [P, S // 16], U16)
         n1_t = tile("n1_t", [P, H // 16], U16)
@@ -62,12 +72,12 @@ def tile_picked_tokfdifsum_none_po_kernel(tc, x_words, x_scales, wa, gt, w1_word
         gt_t = tile("gt_t", [P, PACK], F32)
 
         nc.sync.dma_start(offs_t[:], offs)
+        nc.sync.dma_start(n1_t[:], n1)
         nc.sync.dma_start(out=wa_raw[0][:], in_=wa_rows[:, :, WA_CHUNKS[0][0] : WA_CHUNKS[0][1]])
         load_scale_rows(nc.sync, xs, x_scales[0])
         nc.sync.dma_start(out=xw[:].bitcast(I32), in_=x_words[0].rearrange("p n t -> p (n t)").bitcast(I32))
         for i in range(1, len(WA_CHUNKS)):
             nc.sync.dma_start(out=wa_raw[i][:], in_=wa_rows[:, :, WA_CHUNKS[i][0] : WA_CHUNKS[i][1]])
-        nc.sync.dma_start(n1_t[:], n1)
         nc.sync.dma_start(out=w1w[:].bitcast(I32), in_=w1_words[0].rearrange("p n t -> p (n t)").bitcast(I32))
         load_scale_rows(nc.sync, w1s, w1_scales[0])
         nc.sync.dma_start(out=gt_t[:], in_=gt.rearrange("(p t) o -> p (t o)", t=PACK))
@@ -85,108 +95,114 @@ def tile_picked_tokfdifsum_none_po_kernel(tc, x_words, x_scales, wa, gt, w1_word
         wa_q = tile("wa_q", [P, H], U32)
         wa_s = tile("wa_s", [P, H], U8)
         y_ps = [ps.tile([P, H], F32, name=f"y_ps{t}", tag=f"bank{t}") for t in range(PACK)]
+        y0_tail = ps.tile([P, H - TAIL], F32, name="y0_tail", tag="bank7")
         for i, (c0, c1) in enumerate(WA_CHUNKS):
             wa_bf = tile(f"wa_bf{i}", [P, c1 - c0, PACK], BF16)
-            src = wa_raw[i][:].rearrange("p j c -> p c j")
-            if i == len(WA_CHUNKS) - 1:
-                nc.vector.tensor_copy(wa_bf[:], src)
-            else:
-                nc.scalar.copy(wa_bf[:], src)
-            nc.vector.quantize_mx(out=wa_q[:, c0:c1].bitcast(FP8X4), scales=wa_s[:, c0:c1], in_=wa_bf[:].rearrange("p c j -> p (c j)"))
-            nc.tensor.matmul_mx(out=y_ps[0][:, c0:c1], lhsT=xg[:, 0, :].bitcast(FP8X4), lhsT_scale=xsd[:, 0, :],
-                                rhs=wa_q[:, c0:c1].bitcast(FP8X4), rhs_scale=wa_s[:, c0:c1], start=True, stop=True)
-        for t in range(1, PACK):
-            nc.tensor.matmul_mx(out=y_ps[t][:], lhsT=xg[:, t, :].bitcast(FP8X4), lhsT_scale=xsd[:, t, :],
-                                rhs=wa_q[:].bitcast(FP8X4), rhs_scale=wa_s[:], start=True, stop=True)
+            interleave(nc.vector.tensor_copy if i == len(WA_CHUNKS) - 1 else nc.scalar.copy, wa_bf, wa_raw[i])
+            quantize(wa_q[:, c0:c1], wa_s[:, c0:c1], wa_bf)
+        for t in range(2):
+            for c0, c1 in CHUNKS[:2]:
+                mx(y_ps[t][:, c0:c1], xg[:, t, :], xsd[:, t, :], wa_q[:, c0:c1], wa_s[:, c0:c1])
+        mx(y0_tail[:], xg[:, 0, :], xsd[:, 0, :], wa_q[:, TAIL:H], wa_s[:, TAIL:H])
+        mx(y_ps[1][:, TAIL:H], xg[:, 1, :], xsd[:, 1, :], wa_q[:, TAIL:H], wa_s[:, TAIL:H])
+        for t in range(2, PACK):
+            mx(y_ps[t][:], xg[:, t, :], xsd[:, t, :], wa_q[:], wa_s[:])
 
         w1wd = tile("w1wd", [P, PACK, P], U32)
         w1sd = tile("w1sd", [P, PACK, P], U8)
         nc.vector.tensor_copy(w1wd[:].bitcast(I32).rearrange("p t s -> p s t"), w1w[:].bitcast(I32).rearrange("p (s t) -> p s t", t=PACK))
         nc.vector.tensor_copy(w1sd[:].rearrange("p t s -> p s t"), w1s[:].rearrange("p (s t) -> p s t", t=PACK))
 
-        y = [tile(f"y{t}", [P, H], F32) for t in range(PACK)]
-        y2 = [tile(f"y2_{t}", [P, H], F32) for t in range(PACK)]
+        y_th = [tile(f"y_th{t}", [P, 2 * H], F32) for t in range(PACK)]
         gy = [tile(f"gy{t}", [P, H], F32) for t in range(PACK)]
+        y2 = [tile(f"y2_{t}", [P, H], F32) for t in range(PACK)]
         d = [tile(f"d{t}", [P, H], F32) for t in range(PACK)]
-        th = [tile(f"th{t}", [P, H], F32) for t in range(PACK)]
+        y = [y_th[t][:, 0:H] for t in range(PACK)]
+        th = [y_th[t][:, H : 2 * H] for t in range(PACK)]
         for t in range(PACK):
-            nc.scalar.copy(y[t][:], y_ps[t][:])
+            if t == 0:
+                for dst in (y[0], y2[0]):
+                    nc.scalar.copy(dst[:, 0:TAIL], y_ps[0][:, 0:TAIL])
+                for dst in (y[0], y2[0]):
+                    nc.scalar.copy(dst[:, TAIL:H], y0_tail[:])
+            else:
+                nc.scalar.copy(y[t], y_ps[t][:])
+                nc.scalar.copy(y2[t][:], y_ps[t][:])
+            nc.vector.tensor_tensor(d[t][:], y_th[t][:].indirect(n1_t[:]), y2[t][:], ALU.subtract)
         for t in range(PACK):
-            nc.vector.tensor_copy(y2[t][:], y[t][:])
-            for c0, c1 in HALVES:
-                nc.vector.tensor_tensor(d[t][:, c0:c1], y[t][:].indirect(entries(n1_t, c0, c1)), y2[t][:, c0:c1], ALU.subtract)
+            nc.scalar.activation(gy[t][:], y2[t][:], ACT.Copy, scale=gt_t[:, t : t + 1])
+            nc.scalar.activation(th[t][:, 0:256], d[t][:, 0:256], ACT.Tanh, bias=tanh_bias[:])
         for t in range(PACK):
-            nc.scalar.activation(gy[t][:], y[t][:], ACT.Copy, scale=gt_t[:, t : t + 1])
-            nc.scalar.activation(th[t][:], d[t][:], ACT.Tanh, bias=tanh_bias[:])
+            nc.scalar.activation(th[t][:, 256:H], d[t][:, 256:H], ACT.Tanh, bias=tanh_bias[:])
 
         z_q = tile("z_q", [P, H], U32)
         z_s = tile("z_s", [P, H], U8)
-        h = [tile(f"h{t}", [P, H], F32) for t in range(PACK)]
         ha = [ps.tile([P, 2, 256], F32, name=f"ha{u}", tag=f"bank{4 + u}") for u in range(2)]
         hb = ps.tile([P, PACK, 128], F32, name="hb", tag="bank6")
         hc = [ps.tile([P, 128], F32, name=f"hc{t}", tag=f"bank{t}") for t in range(PACK)]
         h_ps = [[ha[t // 2][:, t % 2, :] for t in range(PACK)], [hb[:, t, :] for t in range(PACK)], [hc[t][:] for t in range(PACK)]]
-
-        z = [tile(f"z{i}", [P, PACK, c1 - c0], F32) for i, (c0, c1) in enumerate(CHUNKS)]
-        z_bf = [tile(f"z_bf{i}", [P, c1 - c0, PACK], BF16) for i, (c0, c1) in enumerate(CHUNKS)]
+        z, z_bf = [], []
+        last = len(CHUNKS) - 1
 
         def finish_z(i):
             c0, c1 = CHUNKS[i]
-            nc.vector.quantize_mx(out=z_q[:, c0:c1].bitcast(FP8X4), scales=z_s[:, c0:c1], in_=z_bf[i][:].rearrange("p c j -> p (c j)"))
+            quantize(z_q[:, c0:c1], z_s[:, c0:c1], z_bf[i])
             for t in range(PACK):
-                nc.tensor.matmul_mx(out=h_ps[i][t], lhsT=w1wd[:, t, :].bitcast(FP8X4), lhsT_scale=w1sd[:, t, :],
-                                    rhs=z_q[:, c0:c1].bitcast(FP8X4), rhs_scale=z_s[:, c0:c1], start=True, stop=True)
+                mx(h_ps[i][t], w1wd[:, t, :], w1sd[:, t, :], z_q[:, c0:c1], z_s[:, c0:c1])
 
-        last = len(CHUNKS) - 1
         for i, (c0, c1) in enumerate(CHUNKS):
+            if i == last:
+                finish_z(0)
+            z.append(tile(f"z{i}", [P, PACK, c1 - c0], F32, tag="zshare0" if i == last else ""))
             for t in range(PACK):
                 nc.vector.tensor_tensor(z[i][:, t, :], gy[t][:].indirect(entries(n2_t, c0, c1)), th[t][:, c0:c1], ALU.mult)
-            src = z[i][:].rearrange("p j c -> p c j")
-            if i > 0:
-                finish_z(i - 1)
             if i == last:
-                nc.vector.tensor_copy(z_bf[i][:], src)
-            else:
-                nc.scalar.copy(z_bf[i][:], src)
+                finish_z(1)
+            z_bf.append(tile(f"z_bf{i}", [P, c1 - c0, PACK], BF16, tag="zshare0" if i == 0 else "zshare1"))
+            interleave(nc.vector.tensor_copy if i == last else nc.scalar.copy, z_bf[i], z[i])
         finish_z(last)
-        for t in range(PACK):
-            for i, (c0, c1) in enumerate(CHUNKS):
+
+        h = [tile(f"h{t}", [P, H], F32) for t in range(PACK)]
+        for i, (c0, c1) in enumerate(CHUNKS):
+            for t in range(PACK):
                 nc.scalar.copy(h[t][:, c0:c1], h_ps[i][t])
 
         o_q = tile("o_q", [P, H], U32)
         o_s = tile("o_s", [P, H], U8)
         out_rows = out_0.rearrange("(p t) j -> p t j", t=PACK)
         out_words = out_1[0].rearrange("p n t -> p (n t)").bitcast(I32)
-        o = [tile(f"o{i}", [P, PACK, c1 - c0], F32) for i, (c0, c1) in enumerate(CHUNKS)]
-        o_bf = [tile(f"o_bf{i}", [P, c1 - c0, PACK], BF16) for i, (c0, c1) in enumerate(CHUNKS)]
-        g = [tile(f"g{i}", [P, PACK, c1 - c0], F32) for i, (c0, c1) in enumerate(CHUNKS)]
+        o, o_bf = [], []
 
         def finish_o(i):
             c0, c1 = CHUNKS[i]
-            nc.vector.quantize_mx(out=o_q[:, c0:c1].bitcast(FP8X4), scales=o_s[:, c0:c1], in_=o_bf[i][:].rearrange("p c j -> p (c j)"))
+            quantize(o_q[:, c0:c1], o_s[:, c0:c1], o_bf[i])
             nc.sync.dma_start(out=out_words[:, c0:c1], in_=o_q[:, c0:c1].bitcast(I32))
 
+        def scaled(dst, t, c0):
+            nc.vector.tensor_scalar(dst[:, t, :], h[t][:].indirect(entries(n4_t, c0, c0 + 256)), 0.75, 0.0, ALU.mult, ALU.add)
+
         for i, (c0, c1) in enumerate(CHUNKS):
-            def first(t):
-                nc.vector.tensor_scalar(g[i][:, t, :], h[t][:].indirect(entries(n4_t, c0, c1)), 0.75, 0.0, ALU.mult, ALU.add)
-
-            def second(t):
-                nc.vector.tensor_tensor(o[i][:, t, :], h[t][:].indirect(entries(n3_t, c0, c1)), g[i][:, t, :], ALU.add)
-
-            first(0)
-            for t in range(1, PACK):
-                first(t)
-                second(t - 1)
-            if i > 0:
-                finish_o(i - 1)
-            second(PACK - 1)
-            nc.sync.dma_start(out=out_rows[:, :, c0:c1], in_=o[i][:])
-            src = o[i][:].rearrange("p j c -> p c j")
+            if i < last:
+                g = tile(f"g{i}", [P, PACK, 256], F32, tag="g")
+                g0 = c0
+            if i == 1:
+                for t in range(PACK):
+                    scaled(g, t, c0)
             if i == last:
-                nc.vector.tensor_copy(o_bf[i][:], src)
-            else:
-                nc.scalar.copy(o_bf[i][:], src)
+                finish_o(0)
+            o.append(tile(f"o{i}", [P, PACK, c1 - c0], F32, tag="oshare0" if i == last else ""))
+            if i == 0:
+                scaled(g, 0, c0)
+            for t in range(PACK):
+                if i == 0 and t + 1 < PACK:
+                    scaled(g, t + 1, c0)
+                nc.vector.tensor_tensor(o[i][:, t, :], h[t][:].indirect(entries(n3_t, c0, c1)), g[:, t, c0 - g0 : c1 - g0], ALU.add)
+            nc.sync.dma_start(out=out_rows[:, :, c0:c1], in_=o[i][:])
+            if i == last:
+                finish_o(1)
+            o_bf.append(tile(f"o_bf{i}", [P, c1 - c0, PACK], BF16, tag="oshare0" if i == 0 else "oshare1"))
+            interleave(nc.vector.tensor_copy if i == last else nc.scalar.copy, o_bf[i], o[i])
         finish_o(last)
-        for q in range(4):
-            queue = nc.scalar if q < 2 else nc.sync
-            queue.dma_start(out=out_2[0, 4 * q : 4 * q + 4, :].bitcast(I32), in_=o_s[32 * q : 32 * q + 4, :].bitcast(I32))
+        for r in range(4):
+            queue = nc.scalar if r < 2 else nc.sync
+            queue.dma_start(out=out_2[0, r:16:4, :].bitcast(I32), in_=o_s[r:P:32, :].bitcast(I32))

from contextlib import ExitStack

import concourse.mybir as mybir

F32 = mybir.dt.float32
BF16 = mybir.dt.bfloat16
U32 = mybir.dt.uint32
I32 = mybir.dt.int32
U16 = mybir.dt.uint16
U8 = mybir.dt.uint8
FP8X4 = mybir.dt.float8_e4m3fn_x4
ALU = mybir.AluOpType
ACT = mybir.ActivationFunctionType

K, T, S, N, H = 512, 2048, 512, 512, 512
P = 128
PACK = 4
FLOPS = 2 * K * S * H + 2 * S * N * H

WA_CHUNKS = [(0, 128), (128, 256), (256, 384), (384, 512)]
CHUNKS = [(0, 256), (256, 384), (384, 512)]
TAIL = 384


def entries(lst, c0, c1):
    return lst[:, c0 // 16 : c1 // 16]


def load_scale_rows(queue, tile, rows):
    for r in range(4):
        queue.dma_start(out=tile[r:P:32, :].bitcast(I32), in_=rows[r:16:4, :].bitcast(I32))


def interleave(copy, dst, src):
    copy(dst[:].rearrange("p (c i) t -> p c t i", i=4), src[:].rearrange("p t (c i) -> p c t i", i=4))


def tile_picked_tokfdifsum_none_po_kernel(tc, x_words, x_scales, wa, gt, w1_words, w1_scales, offs, n1, n2, n3, n4, out_0, out_1, out_2):
    nc = tc.nc
    with ExitStack() as ctx:
        sb = ctx.enter_context(tc.tile_pool(name="sb", bufs=1))
        ps = ctx.enter_context(tc.psum_pool(name="ps", bufs=1))

        def tile(name, shape, dtype, tag=""):
            return sb.tile(shape, dtype, name=name, align_bytes=64, tag=tag or name)

        def mx(out, lhs_q, lhs_s, rhs_q, rhs_s):
            nc.tensor.matmul_mx(out=out, lhsT=lhs_q.bitcast(FP8X4), lhsT_scale=lhs_s, rhs=rhs_q.bitcast(FP8X4), rhs_scale=rhs_s, start=True, stop=True)

        def quantize(codes, scales, src):
            nc.vector.quantize_mx(out=codes.bitcast(FP8X4), scales=scales, in_=src[:].rearrange("p c t -> p (c t)"))

        offs_t = tile("offs_t", [P, S // 16], U16)
        n1_t = tile("n1_t", [P, H // 16], U16)
        n2_t = tile("n2_t", [P, H // 16], U16)
        n3_t = tile("n3_t", [P, H // 16], U16)
        n4_t = tile("n4_t", [P, H // 16], U16)

        xs = tile("xs", [P, T], U8)
        w1s = tile("w1s", [P, N], U8)
        zero = tile("zero", [P, 1], F32)
        tanh_bias = tile("tanh_bias", [P, 1], F32)
        nc.vector.memset(xs[:].bitcast(I32), 0)
        nc.vector.memset(zero[:], 0.0)
        nc.scalar.activation(tanh_bias[:], zero[:], ACT.Tanh)
        nc.vector.memset(w1s[:].bitcast(I32), 0)

        wa_rows = wa.rearrange("(p j) c -> p j c", j=PACK)
        wa_raw = [tile(f"wa_raw{i}", [P, PACK, c1 - c0], F32) for i, (c0, c1) in enumerate(WA_CHUNKS)]
        xw = tile("xw", [P, T], U32)
        w1w = tile("w1w", [P, N], U32)
        gt_t = tile("gt_t", [P, PACK], F32)

        nc.sync.dma_start(offs_t[:], offs)
        nc.sync.dma_start(n1_t[:], n1)
        nc.sync.dma_start(out=wa_raw[0][:], in_=wa_rows[:, :, WA_CHUNKS[0][0] : WA_CHUNKS[0][1]])
        load_scale_rows(nc.sync, xs, x_scales[0])
        nc.sync.dma_start(out=xw[:].bitcast(I32), in_=x_words[0].rearrange("p n t -> p (n t)").bitcast(I32))
        for i in range(1, len(WA_CHUNKS)):
            nc.sync.dma_start(out=wa_raw[i][:], in_=wa_rows[:, :, WA_CHUNKS[i][0] : WA_CHUNKS[i][1]])
        nc.sync.dma_start(out=w1w[:].bitcast(I32), in_=w1_words[0].rearrange("p n t -> p (n t)").bitcast(I32))
        load_scale_rows(nc.sync, w1s, w1_scales[0])
        nc.sync.dma_start(out=gt_t[:], in_=gt.rearrange("(p t) o -> p (t o)", t=PACK))
        nc.sync.dma_start(n2_t[:], n2)
        nc.sync.dma_start(n4_t[:], n4)
        nc.sync.dma_start(n3_t[:], n3)

        xsg = tile("xsg", [P, S], U8)
        xsd = tile("xsd", [P, PACK, P], U8)
        xg = tile("xg", [P, PACK, P], U32)
        nc.vector.tensor_copy(xsg[:], xs[:].indirect(offs_t[:]))
        nc.vector.tensor_copy(xsd[:].rearrange("p t s -> p s t"), xsg[:].rearrange("p (s t) -> p s t", t=PACK))
        nc.vector.tensor_copy(xg[:].rearrange("p t s -> p s t"), xw[:].indirect(offs_t[:]))

        wa_q = tile("wa_q", [P, H], U32)
        wa_s = tile("wa_s", [P, H], U8)
        y_ps = [ps.tile([P, H], F32, name=f"y_ps{t}", tag=f"bank{t}") for t in range(PACK)]
        y0_tail = ps.tile([P, H - TAIL], F32, name="y0_tail", tag="bank7")
        for i, (c0, c1) in enumerate(WA_CHUNKS):
            wa_bf = tile(f"wa_bf{i}", [P, c1 - c0, PACK], BF16)
            interleave(nc.vector.tensor_copy if i == len(WA_CHUNKS) - 1 else nc.scalar.copy, wa_bf, wa_raw[i])
            quantize(wa_q[:, c0:c1], wa_s[:, c0:c1], wa_bf)
        for t in range(2):
            for c0, c1 in CHUNKS[:2]:
                mx(y_ps[t][:, c0:c1], xg[:, t, :], xsd[:, t, :], wa_q[:, c0:c1], wa_s[:, c0:c1])
        mx(y0_tail[:], xg[:, 0, :], xsd[:, 0, :], wa_q[:, TAIL:H], wa_s[:, TAIL:H])
        mx(y_ps[1][:, TAIL:H], xg[:, 1, :], xsd[:, 1, :], wa_q[:, TAIL:H], wa_s[:, TAIL:H])
        for t in range(2, PACK):
            mx(y_ps[t][:], xg[:, t, :], xsd[:, t, :], wa_q[:], wa_s[:])

        w1wd = tile("w1wd", [P, PACK, P], U32)
        w1sd = tile("w1sd", [P, PACK, P], U8)
        nc.vector.tensor_copy(w1wd[:].bitcast(I32).rearrange("p t s -> p s t"), w1w[:].bitcast(I32).rearrange("p (s t) -> p s t", t=PACK))
        nc.vector.tensor_copy(w1sd[:].rearrange("p t s -> p s t"), w1s[:].rearrange("p (s t) -> p s t", t=PACK))

        y_th = [tile(f"y_th{t}", [P, 2 * H], F32) for t in range(PACK)]
        gy = [tile(f"gy{t}", [P, H], F32) for t in range(PACK)]
        y2 = [tile(f"y2_{t}", [P, H], F32) for t in range(PACK)]
        d = [tile(f"d{t}", [P, H], F32) for t in range(PACK)]
        y = [y_th[t][:, 0:H] for t in range(PACK)]
        th = [y_th[t][:, H : 2 * H] for t in range(PACK)]
        for t in range(PACK):
            if t == 0:
                for dst in (y[0], y2[0]):
                    nc.scalar.copy(dst[:, 0:TAIL], y_ps[0][:, 0:TAIL])
                for dst in (y[0], y2[0]):
                    nc.scalar.copy(dst[:, TAIL:H], y0_tail[:])
            else:
                nc.scalar.copy(y[t], y_ps[t][:])
                nc.scalar.copy(y2[t][:], y_ps[t][:])
            nc.vector.tensor_tensor(d[t][:], y_th[t][:].indirect(n1_t[:]), y2[t][:], ALU.subtract)
        for t in range(PACK):
            nc.scalar.activation(gy[t][:], y2[t][:], ACT.Copy, scale=gt_t[:, t : t + 1])
            nc.scalar.activation(th[t][:, 0:256], d[t][:, 0:256], ACT.Tanh, bias=tanh_bias[:])
        for t in range(PACK):
            nc.scalar.activation(th[t][:, 256:H], d[t][:, 256:H], ACT.Tanh, bias=tanh_bias[:])

        z_q = tile("z_q", [P, H], U32)
        z_s = tile("z_s", [P, H], U8)
        ha = [ps.tile([P, 2, 256], F32, name=f"ha{u}", tag=f"bank{4 + u}") for u in range(2)]
        hb = ps.tile([P, PACK, 128], F32, name="hb", tag="bank6")
        hc = [ps.tile([P, 128], F32, name=f"hc{t}", tag=f"bank{t}") for t in range(PACK)]
        h_ps = [[ha[t // 2][:, t % 2, :] for t in range(PACK)], [hb[:, t, :] for t in range(PACK)], [hc[t][:] for t in range(PACK)]]
        z, z_bf = [], []
        last = len(CHUNKS) - 1

        def finish_z(i):
            c0, c1 = CHUNKS[i]
            quantize(z_q[:, c0:c1], z_s[:, c0:c1], z_bf[i])
            for t in range(PACK):
                mx(h_ps[i][t], w1wd[:, t, :], w1sd[:, t, :], z_q[:, c0:c1], z_s[:, c0:c1])

        for i, (c0, c1) in enumerate(CHUNKS):
            if i == last:
                finish_z(0)
            z.append(tile(f"z{i}", [P, PACK, c1 - c0], F32, tag="zshare0" if i == last else ""))
            for t in range(PACK):
                nc.vector.tensor_tensor(z[i][:, t, :], gy[t][:].indirect(entries(n2_t, c0, c1)), th[t][:, c0:c1], ALU.mult)
            if i == last:
                finish_z(1)
            z_bf.append(tile(f"z_bf{i}", [P, c1 - c0, PACK], BF16, tag="zshare0" if i == 0 else "zshare1"))
            interleave(nc.vector.tensor_copy if i == last else nc.scalar.copy, z_bf[i], z[i])
        finish_z(last)

        h = [tile(f"h{t}", [P, H], F32) for t in range(PACK)]
        for i, (c0, c1) in enumerate(CHUNKS):
            for t in range(PACK):
                nc.scalar.copy(h[t][:, c0:c1], h_ps[i][t])

        o_q = tile("o_q", [P, H], U32)
        o_s = tile("o_s", [P, H], U8)
        out_rows = out_0.rearrange("(p t) j -> p t j", t=PACK)
        out_words = out_1[0].rearrange("p n t -> p (n t)").bitcast(I32)
        o, o_bf = [], []

        def finish_o(i):
            c0, c1 = CHUNKS[i]
            quantize(o_q[:, c0:c1], o_s[:, c0:c1], o_bf[i])
            nc.sync.dma_start(out=out_words[:, c0:c1], in_=o_q[:, c0:c1].bitcast(I32))

        def scaled(dst, t, c0):
            nc.vector.tensor_scalar(dst[:, t, :], h[t][:].indirect(entries(n4_t, c0, c0 + 256)), 0.75, 0.0, ALU.mult, ALU.add)

        for i, (c0, c1) in enumerate(CHUNKS):
            if i < last:
                g = tile(f"g{i}", [P, PACK, 256], F32, tag="g")
                g0 = c0
            if i == 1:
                for t in range(PACK):
                    scaled(g, t, c0)
            if i == last:
                finish_o(0)
            o.append(tile(f"o{i}", [P, PACK, c1 - c0], F32, tag="oshare0" if i == last else ""))
            if i == 0:
                scaled(g, 0, c0)
            for t in range(PACK):
                if i == 0 and t + 1 < PACK:
                    scaled(g, t + 1, c0)
                nc.vector.tensor_tensor(o[i][:, t, :], h[t][:].indirect(entries(n3_t, c0, c1)), g[:, t, c0 - g0 : c1 - g0], ALU.add)
            nc.sync.dma_start(out=out_rows[:, :, c0:c1], in_=o[i][:])
            if i == last:
                finish_o(1)
            o_bf.append(tile(f"o_bf{i}", [P, c1 - c0, PACK], BF16, tag="oshare0" if i == 0 else "oshare1"))
            interleave(nc.vector.tensor_copy if i == last else nc.scalar.copy, o_bf[i], o[i])
        finish_o(last)
        for r in range(4):
            queue = nc.scalar if r < 2 else nc.sync
            queue.dma_start(out=out_2[0, r:16:4, :].bitcast(I32), in_=o_s[r:P:32, :].bitcast(I32))
